import numpy as np
import ml_dtypes


def mxq(x, axis, fmt="e4m3"):
    dtype, down = {"e4m3": (ml_dtypes.float8_e4m3fn, 7), "e5m2": (ml_dtypes.float8_e5m2, 14)}[fmt]
    v = np.moveaxis(np.asarray(x, np.float32).astype(ml_dtypes.bfloat16).astype(np.float64), axis, -1)
    blocks = v.reshape(v.shape[:-1] + (-1, 32))
    amax = np.abs(blocks).max(-1, keepdims=True)
    byte = np.maximum(np.where(amax > 0, np.frexp(amax)[1] - 1 + 127, 0) - down, 1)
    scale = np.exp2(byte - 127.0)
    codes = (blocks / scale).astype(np.float32).astype(dtype).astype(np.float64)
    return np.moveaxis((codes * scale).reshape(v.shape), -1, axis)


WIDE = False


def mx_kscale(k):
    if not WIDE:
        return np.ones(k)
    levels = np.array([10, -10, 5, -5, 0])
    if k % 512:
        return np.exp2(np.random.permutation(np.resize(levels, k // 32))).repeat(32)
    a = np.empty((k // 512, 16))
    for p in range(k // 512):
        a[p, :8] = np.random.permutation(np.resize(levels, 8))
        for g in range(8):
            far = levels[np.abs(levels - a[p, g]) >= 10]
            a[p, g + 8] = far[np.random.randint(len(far))]
    return np.exp2(a.ravel()).repeat(32)


def f64(x):
    return np.asarray(x).astype(np.float64)


def striped(idx):
    return np.tile(idx.reshape(-1, 16).T, (8, 1)).astype(np.uint16)


def unstriped(offs):
    return offs[:16].T.reshape(-1).astype(np.int64)


E2M1 = np.array([0.0, 0.5, 1.0, 1.5, 2.0, 3.0, 4.0, 6.0, -0.0, -0.5, -1.0, -1.5, -2.0, -3.0, -4.0, -6.0])


def pack_weight(w, fmt):
    k, n = w.shape
    w = f64(np.asarray(w, np.float32).astype(ml_dtypes.bfloat16)).reshape(k // 32, 32, n)
    amax = np.abs(w).max(1)
    if fmt == "e4m3":
        byte = np.frexp(amax)[1] - 1 + 127 - 7
    else:
        mant, ex = np.frexp(amax / 6.0)
        byte = np.where(mant > 0.5, ex, ex - 1) + 127
    byte = np.clip(np.where(amax > 0, byte, 1), 1, 254)
    scaled = (w * np.exp2(127.0 - byte)[:, None, :]).reshape(k, n).astype(np.float32)
    by_word = np.ascontiguousarray(scaled.reshape(k // 512, 128, 4, n).transpose(0, 1, 3, 2))
    if fmt == "e4m3":
        words = by_word.astype(ml_dtypes.float8_e4m3fn).view(np.uint8)
    else:
        c = by_word.astype(ml_dtypes.float4_e2m1fn).view(np.uint8) & 0xF
        words = (c[..., 0::2] | (c[..., 1::2] << 4)).reshape(k // 512, 128, 2 * n)
    return np.ascontiguousarray(words), np.ascontiguousarray(byte.astype(np.uint8).reshape(k // 512, 16, n))


def unpack_weight(words, scales, fmt):
    g, _, n = scales.shape
    words = np.ascontiguousarray(words).reshape(g, 128, n, -1)
    if fmt == "e4m3":
        vals = words.view(ml_dtypes.float8_e4m3fn).astype(np.float64)
    else:
        nib = np.empty((g, 128, n, 4), np.uint8)
        nib[..., 0::2] = words & 0xF
        nib[..., 1::2] = words >> 4
        vals = E2M1[nib]
    vals = vals * np.repeat(np.exp2(scales.astype(np.float64) - 127.0), 8, axis=1)[..., None]
    return vals.transpose(0, 1, 3, 2).reshape(g * 512, n)


def gelu(v):
    return 0.5 * v * (1.0 + np.tanh(np.sqrt(2.0 / np.pi) * (v + 0.044715 * v**3)))


K, T, H, S, T2, P, N = 1024, 4096, 1024, 1024, 2048, 1024, 512


def setup_inputs():
    n = np.random.standard_normal
    s = mx_kscale(K)[:, None]
    u = mx_kscale(H)[:, None]
    tab_words, tab_scales = pack_weight(n((K, T)) * s, "e4m3")
    w4_words, w4_scales = pack_weight(0.3 * n((K, H)) / np.sqrt(K) / s, "e2m1")
    return {
        "tab_words": tab_words, "tab_scales": tab_scales,
        "offs": striped(np.random.permutation(T)[:S]),
        "w4_words": w4_words, "w4_scales": w4_scales,
        "base": np.random.uniform(-1.3, 1.3, (H, S)).astype(np.float32),
        "gain": (2.2 * np.exp(0.3 * n(H)) * u[:, 0]).astype(np.float32),
        "wgs": np.exp(0.3 * n((128, S))).astype(np.float32),
        "page0": (n((H, T2)) * u).astype(np.float32),
        "offs2": striped(np.random.permutation(T2)[:S]),
        "offs3": striped(np.random.permutation(T2)[:P]),
        "offs4": striped(np.random.permutation(T2)[:P]),
        "w2": (n((H, N)) / np.sqrt(H) / u).astype(np.float32),
        "sens": (0.6 * np.exp(0.3 * n(N))).astype(np.float32),
    }


def reference(tab_words, tab_scales, offs, w4_words, w4_scales, base, gain, wgs, page0, offs2, offs3, offs4, w2, sens):
    v = unpack_weight(tab_words, tab_scales, "e4m3")[:, unstriped(offs)]
    w4 = unpack_weight(w4_words, w4_scales, "e2m1")
    h = f64(gain)[:, None] * np.sin((w4.T @ v) + f64(base))
    before = f64(page0)
    page = before.copy()
    page[:, unstriped(offs2)] = np.tile(f64(wgs), (H // 128, 1)) * h
    x = np.abs(page[:, unstriped(offs3)]) + before[:, unstriped(offs4)]
    y = mxq(f64(w2), 0, "e4m3").T @ mxq(x, 0, "e4m3")
    return np.tanh(y * f64(sens)[:, None])

@@ -1,0 +1,274 @@
+import math
+from contextlib import ExitStack
+
+import concourse.mybir as mybir
+from concourse.masks import make_identity
+
+K, T, H, S, T2, M, N = 1024, 4096, 1024, 1024, 2048, 1024, 512
+FLOPS = 2 * K * H * S + 2 * H * N * M
+
+F32 = mybir.dt.float32
+BF16 = mybir.dt.bfloat16
+I32 = mybir.dt.int32
+U32 = mybir.dt.uint32
+U16 = mybir.dt.uint16
+U8 = mybir.dt.uint8
+FP8X4 = mybir.dt.float8_e4m3fn_x4
+FP4X4 = mybir.dt.float4_e2m1fn_x4
+ACT = mybir.ActivationFunctionType
+MULT = mybir.AluOpType.mult
+
+P = 128
+BANK = 512
+PASSES = 2
+TILES = H // P
+TILES_A_PASS = TILES // PASSES
+N_TILES = N // P
+CHUNK = 256
+CHUNKS = M // CHUNK
+ROUNDER = 12582912.0
+BASE_BUFS = 4
+SINE_BUFS = 3
+OLD_BUFS = 4
+LAG = 2
+
+
+def tile_list_facade_leakage_rounds_kernel(
+    tc, tab_words, tab_scales, offs, w4_words, w4_scales, base, gain, wgs, page0, offs2, offs3, offs4, w2, sens, out
+):
+    nc = tc.nc
+    with ExitStack() as ctx:
+        lists = ctx.enter_context(tc.tile_pool(name="lists", bufs=1))
+        keep = ctx.enter_context(tc.tile_pool(name="keep", bufs=1))
+        psum = ctx.enter_context(tc.psum_pool(name="psum", bufs=1))
+
+        def sb(name, shape, dtype, tag=""):
+            return keep.tile(shape, dtype, name=name, tag=tag or name, align_bytes=64)
+
+        pick = lists.tile([P, S // 16], U16, name="pick")
+        put = lists.tile([P, S // 16], U16, name="put")
+        new_cols = lists.tile([P, M // 16], U16, name="new_cols")
+        old_cols = lists.tile([P, M // 16], U16, name="old_cols")
+
+        banks = [psum.tile([P, BANK], F32, name="bank%d" % b, tag="bank%d" % b) for b in range(8)]
+        acc, summed, reduced, xsum = banks[0:2], banks[2:4], banks[4:6], banks[6:8]
+
+        tab_w = [sb("tab_w%d" % a, [P, T], U32) for a in range(PASSES)]
+        tab_s = sb("tab_s", [P, PASSES, T], U8)
+        v_s = sb("v_s", [P, PASSES, S], U8)
+        w4_w = sb("w4_w", [P, PASSES, 2 * H], U8)
+        w4_s = sb("w4_s", [P, PASSES, H], U8)
+        ident = sb("ident", [P, P], F32)
+        vec_rows = sb("vec_rows", [P, P], F32)
+        gain_cols = sb("gain_cols", [P, TILES], F32)
+        sens_cols = sb("sens_cols", [P, N_TILES], F32)
+        x_g = sb("x_g", [P, M, 4], BF16)
+        x_w = sb("x_w", [P, PASSES, M], U32)
+        wgs_sb = sb("wgs_sb", [P, S], F32)
+        pages = [sb("page%d" % c, [P, T2], F32) for c in range(TILES)]
+        bases = [sb("base%d" % b, [P, S], F32) for b in range(BASE_BUFS)]
+        factors = [sb("factor%d" % c, [P, S], F32) for c in range(TILES)]
+        sines = [sb("sine%d" % b, [P, S], F32) for b in range(SINE_BUFS)]
+        prod = [sb("prod%d" % h, [P, BANK], F32) for h in range(2)]
+        turns = [sb("turns%d" % h, [P, BANK], F32) for h in range(2)]
+        whole = [sb("whole%d" % h, [P, BANK], U32) for h in range(2)]
+        addend = [sb("addend%d" % h, [P, BANK], F32) for h in range(2)]
+        x_t = [sb("x_t%d" % q, [P, 2, 2, P, 2], BF16) for q in range(CHUNKS)]
+        x_s = sb("x_s", [P, PASSES, M], U8)
+        w2_g = sb("w2_g", [P, N, 4], BF16)
+        w2_w = sb("w2_w", [P, PASSES, N], U32)
+        w2_s = sb("w2_s", [P, PASSES, N], U8)
+
+        def load_base(c):
+            nc.sync.dma_start(bases[c % BASE_BUFS][:], base[c * P : (c + 1) * P, :])
+
+        def load_page(c):
+            nc.sync.dma_start(pages[c][:], page0[c * P : (c + 1) * P, :])
+
+        def load_w4(cols):
+            nc.sync.dma_start(w4_w[:, :, cols].bitcast(I32), w4_words[:, :, cols].rearrange("a p c -> p a c").bitcast(I32))
+
+        nc.gpsimd.memset(vec_rows[:], 0.0)
+        nc.vector.memset(tab_s[:].rearrange("p a t -> p (a t)").bitcast(I32), 0)
+        nc.vector.memset(w4_s[:].rearrange("p a t -> p (a t)").bitcast(I32), 0)
+        nc.gpsimd.dma_start(vec_rows[0:TILES, :], gain.rearrange("(c p) -> c p", p=P))
+        make_identity(nc, ident[:])
+        for scales_sb, scales in ((tab_s, tab_scales), (w4_s, w4_scales)):
+            for quad in range(4):
+                nc.gpsimd.dma_start(
+                    scales_sb[32 * quad : 32 * quad + 4, :, :].bitcast(I32),
+                    scales[:, 4 * quad : 4 * quad + 4, :].rearrange("a q t -> q a t").bitcast(I32),
+                )
+        nc.sync.dma_start(pick[:], offs)
+        nc.sync.dma_start(wgs_sb[:], wgs)
+        for a in range(PASSES):
+            nc.sync.dma_start(tab_w[a][:].bitcast(I32), tab_words[a].rearrange("p t i -> p (t i)").bitcast(I32))
+        load_w4(slice(0, 2 * P))
+        load_base(0)
+        nc.sync.dma_start(old_cols[:], offs4)
+        load_page(0)
+        nc.sync.dma_start(put[:], offs2)
+        load_w4(slice(2 * P, 2 * H))
+        load_base(1)
+        load_page(1)
+        nc.sync.dma_start(new_cols[:], offs3)
+        for c in range(2, BASE_BUFS):
+            load_page(c)
+            load_base(c)
+
+        nc.tensor.transpose(xsum[0][:, 0:P], vec_rows[:], ident[:])
+        nc.scalar.copy(gain_cols[:], xsum[0][:, 0:TILES])
+        for c in range(TILES):
+            nc.scalar.activation(factors[c][:], wgs_sb[:], ACT.Copy, scale=gain_cols[:, c : c + 1])
+
+        for a in range(PASSES):
+            nc.vector.tensor_copy(v_s[:, a, :], tab_s[:, a, :].indirect(pick[:]))
+        v_w = sb("v_w", [P, PASSES, S], U32, tag="tab_s")
+        nc.vector.tensor_copy(v_w[:, 0, :], tab_w[0][:].indirect(pick[:]))
+        for h in range(2):
+            nc.vector.tensor_copy(
+                v_w[:, 1, h * BANK : (h + 1) * BANK], tab_w[1][:].indirect(pick[:, h * BANK // 16 : (h + 1) * BANK // 16])
+            )
+
+        def add_transposed(bank, first, second, blocks):
+            for i, src in enumerate((first, second)):
+                for b in range(blocks):
+                    cols = slice(b * P, (b + 1) * P)
+                    nc.tensor.matmul(
+                        bank[:, cols], src[:, cols], ident[:], is_transpose=True,
+                        start=(i == 0 and b == 0), stop=(i == 1 and b == blocks - 1),
+                    )
+
+        def first_stage(c):
+            halves = [slice(h * BANK, (h + 1) * BANK) for h in range(2)]
+            for h in range(2):
+                for a in range(PASSES):
+                    nc.tensor.matmul_mx(
+                        acc[h][:],
+                        lhsT=w4_w[:, a, 2 * c * P : 2 * (c + 1) * P].bitcast(FP4X4),
+                        lhsT_scale=w4_s[:, a, c * P : (c + 1) * P],
+                        rhs=v_w[:, a, halves[h]].bitcast(FP8X4),
+                        rhs_scale=v_s[:, a, halves[h]],
+                        start=(a == 0), stop=(a == PASSES - 1),
+                    )
+                nc.scalar.copy(prod[h][:], acc[h][:])
+                add_transposed(summed[h], bases[c % BASE_BUFS][:, halves[h]], prod[h], 4)
+                nc.scalar.activation(whole[h][:], summed[h][:], ACT.Copy, bias=ROUNDER, scale=0.5 / math.pi)
+                nc.scalar.activation(turns[h][:], summed[h][:], ACT.Copy, scale=0.5 / math.pi)
+                nc.scalar.activation(addend[h][:], whole[h][:], ACT.Copy, bias=ROUNDER, scale=-1.0)
+                add_transposed(reduced[h], turns[h], addend[h], 4)
+                nc.scalar.activation(sines[c % SINE_BUFS][:, halves[h]], reduced[h][:], ACT.Sin, scale=2.0 * math.pi)
+
+        def fetch_old(c):
+            nc.vector.tensor_copy(olds[:, c % OLD_BUFS, :], pages[c][:].indirect(old_cols[:]))
+
+        def put_new(c):
+            pieces = 2 if c == 0 else 1
+            for h in range(pieces):
+                cols = slice(h * S // pieces, (h + 1) * S // pieces)
+                nc.vector.tensor_tensor(
+                    pages[c][:].indirect(put[:, cols.start // 16 : cols.stop // 16]),
+                    sines[c % SINE_BUFS][:, cols], factors[c][:, cols], MULT,
+                )
+
+        def round_x(c, q, sums):
+            rows = slice(32 * (c % TILES_A_PASS), 32 * (c % TILES_A_PASS) + 32)
+            nc.scalar.copy(x_t[q][:, :, :, rows, :], sums.rearrange("p (b i u e) -> p b u i e", b=2, u=2, e=2))
+
+        def second_stage(c):
+            for h in range(2):
+                cols = slice(h * BANK, (h + 1) * BANK)
+                nc.scalar.activation(addend[h][:], factors[c][:, cols], ACT.Abs)
+                add_transposed(xsum[h], addend[h], olds[:, c % OLD_BUFS, cols], 4)
+            for q in range(CHUNKS):
+                round_x(c, q, xsum[q // 2][:, (q % 2) * CHUNK : (q % 2 + 1) * CHUNK])
+
+        def turn_x(q, bank, x_g, copy):
+            words = x_t[q][:].rearrange("p b u i e -> p (b u i e)").bitcast(F32)
+            for blk in range(4):
+                nc.tensor.transpose(bank[:, blk * P : (blk + 1) * P], words[:, blk * P : (blk + 1) * P], ident[:])
+            dst = x_g[:, q * CHUNK : (q + 1) * CHUNK, :].rearrange("p m t -> p (m t)").bitcast(F32)
+            copy(dst.rearrange("p (b m u) -> p b m u", b=2, u=2), bank[:].rearrange("p (b u m) -> p b m u", b=2, u=2))
+
+        def quantise_x(a, cols, x_g, x_w):
+            nc.vector.quantize_mx(
+                out=x_w[:, a, cols].bitcast(FP8X4), scales=x_s[:, a, cols], in_=x_g[:, cols, :].rearrange("p m t -> p (m t)")
+            )
+
+        def quantise_w2():
+            raw = sb("w2_raw", [P, PASSES, 4, N], F32, tag="tab_w0")
+            for a in range(PASSES):
+                nc.sync.dma_start(raw[:, a, :, :], w2[a * BANK : (a + 1) * BANK, :].rearrange("(p t) n -> p t n", t=4))
+            for a in range(PASSES):
+                nc.scalar.copy(
+                    w2_g[:].rearrange("p (c i) t -> p c t i", i=4), raw[:, a, :, :].rearrange("p t (c i) -> p c t i", i=4)
+                )
+                nc.vector.quantize_mx(
+                    out=w2_w[:, a, :].bitcast(FP8X4), scales=w2_s[:, a, :], in_=w2_g[:].rearrange("p n t -> p (n t)")
+                )
+
+        olds = sb("olds", [P, OLD_BUFS, M], F32, tag="tab_w1")
+        for c in range(OLD_BUFS):
+            fetch_old(c)
+        for c in range(TILES + LAG - 1):
+            if c < TILES:
+                first_stage(c)
+                if c + BASE_BUFS < TILES:
+                    load_base(c + BASE_BUFS)
+                    load_page(c + BASE_BUFS)
+                put_new(c)
+            if c < TILES - 1:
+                nc.vector.tensor_copy(factors[c][:], pages[c][:].indirect(new_cols[:]))
+            if c >= LAG:
+                second_stage(c - LAG)
+                if c - LAG + OLD_BUFS < TILES:
+                    fetch_old(c - LAG + OLD_BUFS)
+                if c - LAG == TILES_A_PASS - 1:
+                    for q in range(CHUNKS):
+                        turn_x(q, xsum[q % 2], x_g, nc.scalar.copy)
+                    quantise_x(0, slice(0, M), x_g, x_w)
+            if c == TILES_A_PASS - 1:
+                quantise_w2()
+                with nc.allow_non_contiguous_dma(reason="one factor a partition"):
+                    nc.sync.dma_start(sens_cols[:], sens.rearrange("(t p) -> p t", p=P))
+
+        last = TILES - 1
+        for q in range(CHUNKS):
+            cols = slice(q * CHUNK, (q + 1) * CHUNK)
+            nc.vector.tensor_copy(
+                factors[last][:, cols], pages[last][:].indirect(new_cols[:, q * CHUNK // 16 : (q + 1) * CHUNK // 16])
+            )
+        for q in range(CHUNKS):
+            cols = slice(q * CHUNK, (q + 1) * CHUNK)
+            size = addend[q // 2][:, (q % 2) * CHUNK : (q % 2 + 1) * CHUNK]
+            nc.scalar.activation(size, factors[last][:, cols], ACT.Abs)
+            add_transposed(xsum[q % 2], olds[:, last % OLD_BUFS, cols], size, 2)
+            round_x(last, q, xsum[q % 2][:, 0:CHUNK])
+            turn_x(q, reduced[q % 2], x_g, nc.vector.tensor_copy)
+            quantise_x(1, cols, x_g, x_w)
+        for q in range(CHUNKS):
+            cols = slice(q * CHUNK, (q + 1) * CHUNK)
+            staged = sines[q % 2]
+            for pair in range(2):
+                bank = banks[2 * (q % 2) + pair]
+                for a in range(PASSES):
+                    for i in range(2):
+                        n_cols = slice((2 * pair + i) * P, (2 * pair + i + 1) * P)
+                        nc.tensor.matmul_mx(
+                            bank[:, i * CHUNK : (i + 1) * CHUNK],
+                            lhsT=w2_w[:, a, n_cols].bitcast(FP8X4),
+                            lhsT_scale=w2_s[:, a, n_cols],
+                            rhs=x_w[:, a, cols].bitcast(FP8X4),
+                            rhs_scale=x_s[:, a, cols],
+                            start=(a == 0 and i == 0), stop=(a == PASSES - 1 and i == 1),
+                        )
+                for i in range(2):
+                    nt = 2 * pair + i
+                    nc.scalar.activation(
+                        staged[:, nt * CHUNK : (nt + 1) * CHUNK], bank[:, i * CHUNK : (i + 1) * CHUNK], ACT.Tanh,
+                        scale=sens_cols[:, nt : nt + 1],
+                    )
+                nc.sync.dma_start(
+                    out[2 * pair * P : 2 * (pair + 1) * P, cols].rearrange("(i p) m -> p i m", p=P),
+                    staged[:, 2 * pair * CHUNK : 2 * (pair + 1) * CHUNK].rearrange("p (i m) -> p i m", i=2),
+                )

@@ -75,7 +75,7 @@ def tile_list_facade_leakage_rounds_kernel(
         addend = [sb("addend%d" % h, [P, BANK], F32) for h in range(2)]
         x_t = [sb("x_t%d" % q, [P, 2, 2, P, 2], BF16) for q in range(CHUNKS)]
         x_s = sb("x_s", [P, PASSES, M], U8)
-        w2_g = sb("w2_g", [P, N, 4], BF16)
+        w2_g = [sb("w2_g%d" % a, [P, N, 4], BF16) for a in range(PASSES)]
         w2_w = sb("w2_w", [P, PASSES, N], U32)
         w2_s = sb("w2_s", [P, PASSES, N], U8)
 
@@ -88,30 +88,34 @@ def tile_list_facade_leakage_rounds_kernel(
         def load_w4(cols):
             nc.sync.dma_start(w4_w[:, :, cols].bitcast(I32), w4_words[:, :, cols].rearrange("a p c -> p a c").bitcast(I32))
 
+        def load_table(a):
+            nc.sync.dma_start(tab_w[a][:].bitcast(I32), tab_words[a].rearrange("p t i -> p (t i)").bitcast(I32))
+
+        def load_scales(queue, scales_sb, scales):
+            for quad in range(4):
+                queue.dma_start(
+                    scales_sb[32 * quad : 32 * quad + 4, :, :].bitcast(I32),
+                    scales[:, 4 * quad : 4 * quad + 4, :].rearrange("a q t -> q a t").bitcast(I32),
+                )
+
         nc.gpsimd.memset(vec_rows[:], 0.0)
         nc.vector.memset(tab_s[:].rearrange("p a t -> p (a t)").bitcast(I32), 0)
         nc.vector.memset(w4_s[:].rearrange("p a t -> p (a t)").bitcast(I32), 0)
         nc.gpsimd.dma_start(vec_rows[0:TILES, :], gain.rearrange("(c p) -> c p", p=P))
         make_identity(nc, ident[:])
-        for scales_sb, scales in ((tab_s, tab_scales), (w4_s, w4_scales)):
-            for quad in range(4):
-                nc.gpsimd.dma_start(
-                    scales_sb[32 * quad : 32 * quad + 4, :, :].bitcast(I32),
-                    scales[:, 4 * quad : 4 * quad + 4, :].rearrange("a q t -> q a t").bitcast(I32),
-                )
-        nc.sync.dma_start(pick[:], offs)
-        nc.sync.dma_start(wgs_sb[:], wgs)
-        for a in range(PASSES):
-            nc.sync.dma_start(tab_w[a][:].bitcast(I32), tab_words[a].rearrange("p t i -> p (t i)").bitcast(I32))
+        load_scales(nc.gpsimd, w4_s, w4_scales)
+        load_scales(nc.scalar, tab_s, tab_scales)
+        for tile, source in ((pick, offs), (put, offs2), (new_cols, offs3), (old_cols, offs4)):
+            nc.sync.dma_start(tile[:], source)
         load_w4(slice(0, 2 * P))
+        load_table(0)
+        nc.sync.dma_start(wgs_sb[:], wgs)
+        load_table(1)
         load_base(0)
-        nc.sync.dma_start(old_cols[:], offs4)
         load_page(0)
-        nc.sync.dma_start(put[:], offs2)
         load_w4(slice(2 * P, 2 * H))
         load_base(1)
         load_page(1)
-        nc.sync.dma_start(new_cols[:], offs3)
         for c in range(2, BASE_BUFS):
             load_page(c)
             load_base(c)
@@ -121,13 +125,14 @@ def tile_list_facade_leakage_rounds_kernel(
         for c in range(TILES):
             nc.scalar.activation(factors[c][:], wgs_sb[:], ACT.Copy, scale=gain_cols[:, c : c + 1])
 
+        v_w = [sb("v_w0", [P, S], U32)]
+        nc.vector.tensor_copy(v_w[0][:], tab_w[0][:].indirect(pick[:]))
         for a in range(PASSES):
             nc.vector.tensor_copy(v_s[:, a, :], tab_s[:, a, :].indirect(pick[:]))
-        v_w = sb("v_w", [P, PASSES, S], U32, tag="tab_s")
-        nc.vector.tensor_copy(v_w[:, 0, :], tab_w[0][:].indirect(pick[:]))
+        v_w.append(sb("v_w1", [P, S], U32, tag="tab_s"))
         for h in range(2):
             nc.vector.tensor_copy(
-                v_w[:, 1, h * BANK : (h + 1) * BANK], tab_w[1][:].indirect(pick[:, h * BANK // 16 : (h + 1) * BANK // 16])
+                v_w[1][:, h * BANK : (h + 1) * BANK], tab_w[1][:].indirect(pick[:, h * BANK // 16 : (h + 1) * BANK // 16])
             )
 
         def add_transposed(bank, first, second, blocks):
@@ -139,49 +144,59 @@ def tile_list_facade_leakage_rounds_kernel(
                         start=(i == 0 and b == 0), stop=(i == 1 and b == blocks - 1),
                     )
 
-        def first_stage(c):
-            halves = [slice(h * BANK, (h + 1) * BANK) for h in range(2)]
-            for h in range(2):
-                for a in range(PASSES):
-                    nc.tensor.matmul_mx(
-                        acc[h][:],
-                        lhsT=w4_w[:, a, 2 * c * P : 2 * (c + 1) * P].bitcast(FP4X4),
-                        lhsT_scale=w4_s[:, a, c * P : (c + 1) * P],
-                        rhs=v_w[:, a, halves[h]].bitcast(FP8X4),
-                        rhs_scale=v_s[:, a, halves[h]],
-                        start=(a == 0), stop=(a == PASSES - 1),
-                    )
-                nc.scalar.copy(prod[h][:], acc[h][:])
-                add_transposed(summed[h], bases[c % BASE_BUFS][:, halves[h]], prod[h], 4)
-                nc.scalar.activation(whole[h][:], summed[h][:], ACT.Copy, bias=ROUNDER, scale=0.5 / math.pi)
-                nc.scalar.activation(turns[h][:], summed[h][:], ACT.Copy, scale=0.5 / math.pi)
-                nc.scalar.activation(addend[h][:], whole[h][:], ACT.Copy, bias=ROUNDER, scale=-1.0)
-                add_transposed(reduced[h], turns[h], addend[h], 4)
-                nc.scalar.activation(sines[c % SINE_BUFS][:, halves[h]], reduced[h][:], ACT.Sin, scale=2.0 * math.pi)
+        def half_cols(u):
+            return slice((u % 2) * BANK, (u % 2 + 1) * BANK)
+
+        def multiply(u):
+            c, h = divmod(u, 2)
+            for a in range(PASSES):
+                nc.tensor.matmul_mx(
+                    acc[h][:],
+                    lhsT=w4_w[:, a, 2 * c * P : 2 * (c + 1) * P].bitcast(FP4X4),
+                    lhsT_scale=w4_s[:, a, c * P : (c + 1) * P],
+                    rhs=v_w[a][:, half_cols(u)].bitcast(FP8X4),
+                    rhs_scale=v_s[:, a, half_cols(u)],
+                    start=(a == 0), stop=(a == PASSES - 1),
+                )
+            nc.scalar.copy(prod[h][:], acc[h][:])
+            add_transposed(summed[h], bases[c % BASE_BUFS][:, half_cols(u)], prod[h], 4)
+
+        def reduce_range(u):
+            h = u % 2
+            nc.scalar.activation(whole[h][:], summed[h][:], ACT.Copy, bias=ROUNDER, scale=0.5 / math.pi)
+            nc.scalar.activation(turns[h][:], summed[h][:], ACT.Copy, scale=0.5 / math.pi)
+            nc.scalar.activation(addend[h][:], whole[h][:], ACT.Copy, bias=ROUNDER, scale=-1.0)
+            add_transposed(reduced[h], turns[h], addend[h], 4)
+
+        def take_sine(u):
+            c, h = divmod(u, 2)
+            nc.scalar.activation(sines[c % SINE_BUFS][:, half_cols(u)], reduced[h][:], ACT.Sin, scale=2.0 * math.pi)
 
         def fetch_old(c):
             nc.vector.tensor_copy(olds[:, c % OLD_BUFS, :], pages[c][:].indirect(old_cols[:]))
 
-        def put_new(c):
-            pieces = 2 if c == 0 else 1
-            for h in range(pieces):
-                cols = slice(h * S // pieces, (h + 1) * S // pieces)
-                nc.vector.tensor_tensor(
-                    pages[c][:].indirect(put[:, cols.start // 16 : cols.stop // 16]),
-                    sines[c % SINE_BUFS][:, cols], factors[c][:, cols], MULT,
-                )
+        def put_new(c, cols):
+            nc.vector.tensor_tensor(
+                pages[c][:].indirect(put[:, cols.start // 16 : cols.stop // 16]),
+                sines[c % SINE_BUFS][:, cols], factors[c][:, cols], MULT,
+            )
+
+        def fetch_new(c, cols):
+            nc.vector.tensor_copy(factors[c][:, cols], pages[c][:].indirect(new_cols[:, cols.start // 16 : cols.stop // 16]))
 
         def round_x(c, q, sums):
             rows = slice(32 * (c % TILES_A_PASS), 32 * (c % TILES_A_PASS) + 32)
             nc.scalar.copy(x_t[q][:, :, :, rows, :], sums.rearrange("p (b i u e) -> p b u i e", b=2, u=2, e=2))
 
-        def second_stage(c):
-            for h in range(2):
-                cols = slice(h * BANK, (h + 1) * BANK)
-                nc.scalar.activation(addend[h][:], factors[c][:, cols], ACT.Abs)
-                add_transposed(xsum[h], addend[h], olds[:, c % OLD_BUFS, cols], 4)
-            for q in range(CHUNKS):
-                round_x(c, q, xsum[q // 2][:, (q % 2) * CHUNK : (q % 2 + 1) * CHUNK])
+        def sum_x(u):
+            c, h = divmod(u, 2)
+            nc.scalar.activation(addend[h][:], factors[c][:, half_cols(u)], ACT.Abs)
+            add_transposed(xsum[h], addend[h], olds[:, c % OLD_BUFS, half_cols(u)], 4)
+
+        def round_half(u):
+            c, h = divmod(u, 2)
+            for i in range(2):
+                round_x(c, 2 * h + i, xsum[h][:, i * CHUNK : (i + 1) * CHUNK])
 
         def turn_x(q, bank, x_g, copy):
             words = x_t[q][:].rearrange("p b u i e -> p (b u i e)").bitcast(F32)
@@ -201,43 +216,59 @@ def tile_list_facade_leakage_rounds_kernel(
                 nc.sync.dma_start(raw[:, a, :, :], w2[a * BANK : (a + 1) * BANK, :].rearrange("(p t) n -> p t n", t=4))
             for a in range(PASSES):
                 nc.scalar.copy(
-                    w2_g[:].rearrange("p (c i) t -> p c t i", i=4), raw[:, a, :, :].rearrange("p t (c i) -> p c t i", i=4)
+                    w2_g[a][:].rearrange("p (c i) t -> p c t i", i=4), raw[:, a, :, :].rearrange("p t (c i) -> p c t i", i=4)
                 )
                 nc.vector.quantize_mx(
-                    out=w2_w[:, a, :].bitcast(FP8X4), scales=w2_s[:, a, :], in_=w2_g[:].rearrange("p n t -> p (n t)")
+                    out=w2_w[:, a, :].bitcast(FP8X4), scales=w2_s[:, a, :], in_=w2_g[a][:].rearrange("p n t -> p (n t)")
                 )
 
         olds = sb("olds", [P, OLD_BUFS, M], F32, tag="tab_w1")
         for c in range(OLD_BUFS):
             fetch_old(c)
-        for c in range(TILES + LAG - 1):
-            if c < TILES:
-                first_stage(c)
-                if c + BASE_BUFS < TILES:
-                    load_base(c + BASE_BUFS)
-                    load_page(c + BASE_BUFS)
-                put_new(c)
-            if c < TILES - 1:
-                nc.vector.tensor_copy(factors[c][:], pages[c][:].indirect(new_cols[:]))
-            if c >= LAG:
-                second_stage(c - LAG)
-                if c - LAG + OLD_BUFS < TILES:
-                    fetch_old(c - LAG + OLD_BUFS)
-                if c - LAG == TILES_A_PASS - 1:
-                    for q in range(CHUNKS):
-                        turn_x(q, xsum[q % 2], x_g, nc.scalar.copy)
-                    quantise_x(0, slice(0, M), x_g, x_w)
-            if c == TILES_A_PASS - 1:
+        halves = 2 * TILES
+        for u in range(2):
+            multiply(u)
+            reduce_range(u)
+            take_sine(u)
+            put_new(0, half_cols(u))
+        fetch_new(0, slice(0, M))
+        load_base(BASE_BUFS)
+        load_page(BASE_BUFS)
+        for u in range(halves + 2 * LAG - 1):
+            if u + 2 < halves:
+                multiply(u + 2)
+                if u % 2 == 1 and (u + 2) // 2 + BASE_BUFS < TILES:
+                    load_base((u + 2) // 2 + BASE_BUFS)
+                    load_page((u + 2) // 2 + BASE_BUFS)
+            if 2 <= u + 1 < halves:
+                reduce_range(u + 1)
+            if 2 <= u < halves:
+                take_sine(u)
+                if u % 2 == 1:
+                    put_new(u // 2, slice(0, S))
+                    if u // 2 < TILES - 1:
+                        fetch_new(u // 2, slice(0, M))
+            behind = u - 2 * LAG
+            if 0 <= behind - 1 < halves - 2:
+                round_half(behind - 1)
+                if (behind - 1) // 2 == TILES_A_PASS - 1:
+                    h = (behind - 1) % 2
+                    for i in range(2):
+                        turn_x(2 * h + i, xsum[h], x_g, nc.scalar.copy)
+                    if h == 1:
+                        quantise_x(0, slice(0, M), x_g, x_w)
+            if 0 <= behind < halves - 2:
+                sum_x(behind)
+                if behind % 2 == 1 and behind // 2 + OLD_BUFS < TILES:
+                    fetch_old(behind // 2 + OLD_BUFS)
+            if u == 2 * TILES_A_PASS - 1:
                 quantise_w2()
                 with nc.allow_non_contiguous_dma(reason="one factor a partition"):
                     nc.sync.dma_start(sens_cols[:], sens.rearrange("(t p) -> p t", p=P))
 
         last = TILES - 1
         for q in range(CHUNKS):
-            cols = slice(q * CHUNK, (q + 1) * CHUNK)
-            nc.vector.tensor_copy(
-                factors[last][:, cols], pages[last][:].indirect(new_cols[:, q * CHUNK // 16 : (q + 1) * CHUNK // 16])
-            )
+            fetch_new(last, slice(q * CHUNK, (q + 1) * CHUNK))
         for q in range(CHUNKS):
             cols = slice(q * CHUNK, (q + 1) * CHUNK)
             size = addend[q // 2][:, (q % 2) * CHUNK : (q % 2 + 1) * CHUNK]

@@ -17,20 +17,26 @@ FP8X4 = mybir.dt.float8_e4m3fn_x4
 FP4X4 = mybir.dt.float4_e2m1fn_x4
 ACT = mybir.ActivationFunctionType
 MULT = mybir.AluOpType.mult
+ADD = mybir.AluOpType.add
 
 P = 128
 BANK = 512
 PASSES = 2
-TILES = H // P
-TILES_A_PASS = TILES // PASSES
+PACK = 4
+TILES = PASSES * PACK
+HALVES = 2 * TILES
 N_TILES = N // P
 CHUNK = 256
 CHUNKS = M // CHUNK
 ROUNDER = 12582912.0
-BASE_BUFS = 4
+PAGE_BUFS = 4
 SINE_BUFS = 3
-OLD_BUFS = 4
-LAG = 2
+SPARE_X = 2
+
+
+def place(c):
+    a = c // PACK
+    return a, (c + SPARE_X * a) % PACK
 
 
 def tile_list_facade_leakage_rounds_kernel(
@@ -51,42 +57,53 @@ def tile_list_facade_leakage_rounds_kernel(
         old_cols = lists.tile([P, M // 16], U16, name="old_cols")
 
         banks = [psum.tile([P, BANK], F32, name="bank%d" % b, tag="bank%d" % b) for b in range(8)]
-        acc, summed, reduced, xsum = banks[0:2], banks[2:4], banks[4:6], banks[6:8]
+        acc, summed, reduced = banks[0:2], banks[2:4], banks[4:6]
 
         tab_w = [sb("tab_w%d" % a, [P, T], U32) for a in range(PASSES)]
         tab_s = sb("tab_s", [P, PASSES, T], U8)
         v_s = sb("v_s", [P, PASSES, S], U8)
-        w4_w = sb("w4_w", [P, PASSES, 2 * H], U8)
-        w4_s = sb("w4_s", [P, PASSES, H], U8)
+        w4_raw = sb("w4_raw", [P, PASSES, H], U16)
+        w4_raw_s = sb("w4_raw_s", [P, PASSES, H], U8)
+        w4_w = sb("w4_w", [P, PASSES, PASSES, PACK, P], U16)
+        w4_s = sb("w4_s", [P, PASSES, PASSES, PACK, P], U8)
         ident = sb("ident", [P, P], F32)
-        vec_rows = sb("vec_rows", [P, P], F32)
-        gain_cols = sb("gain_cols", [P, TILES], F32)
+        gain_cols = sb("gain_cols", [P, PASSES, PACK], F32)
         sens_cols = sb("sens_cols", [P, N_TILES], F32)
-        x_g = sb("x_g", [P, M, 4], BF16)
-        x_w = sb("x_w", [P, PASSES, M], U32)
-        wgs_sb = sb("wgs_sb", [P, S], F32)
-        pages = [sb("page%d" % c, [P, T2], F32) for c in range(TILES)]
-        bases = [sb("base%d" % b, [P, S], F32) for b in range(BASE_BUFS)]
+        wgs_sb = [sb("wgs%d" % t, [P, S], F32) for t in range(PACK)]
         factors = [sb("factor%d" % c, [P, S], F32) for c in range(TILES)]
         sines = [sb("sine%d" % b, [P, S], F32) for b in range(SINE_BUFS)]
+        bases = [sines[SINE_BUFS - 1]] + factors[1:]
         prod = [sb("prod%d" % h, [P, BANK], F32) for h in range(2)]
-        turns = [sb("turns%d" % h, [P, BANK], F32) for h in range(2)]
         whole = [sb("whole%d" % h, [P, BANK], U32) for h in range(2)]
-        addend = [sb("addend%d" % h, [P, BANK], F32) for h in range(2)]
-        x_t = [sb("x_t%d" % q, [P, 2, 2, P, 2], BF16) for q in range(CHUNKS)]
+        terms = [sb("terms%d" % h, [P, 2 * BANK], F32) for h in range(2)]
+        x_f = sb("x_f", [P, PACK + SPARE_X, M], F32)
+        x_g = sb("x_g", [P, M, PACK], BF16)
+        x_w = sb("x_w", [P, PASSES, M], U32)
         x_s = sb("x_s", [P, PASSES, M], U8)
-        w2_g = [sb("w2_g%d" % a, [P, N, 4], BF16) for a in range(PASSES)]
+        w2_raw = sb("w2_raw", [P, PASSES, PACK, N], F32)
+        w2_g = [sb("w2_g%d" % a, [P, N, PACK], BF16) for a in range(PASSES)]
         w2_w = sb("w2_w", [P, PASSES, N], U32)
         w2_s = sb("w2_s", [P, PASSES, N], U8)
+        pages, befores = {}, {}
+
+        def rows_of(matrix, c):
+            a, t = place(c)
+            return matrix.rearrange("(a p t) j -> a t p j", a=PASSES, t=PACK)[a, t]
 
         def load_base(c):
-            nc.sync.dma_start(bases[c % BASE_BUFS][:], base[c * P : (c + 1) * P, :])
+            nc.sync.dma_start(bases[c][:], rows_of(base, c))
 
         def load_page(c):
-            nc.sync.dma_start(pages[c][:], page0[c * P : (c + 1) * P, :])
+            pages[c] = sb("page%d" % c, [P, T2], F32, tag="page%d" % (c % PAGE_BUFS))
+            nc.sync.dma_start(pages[c][:], rows_of(page0, c))
 
-        def load_w4(cols):
-            nc.sync.dma_start(w4_w[:, :, cols].bitcast(I32), w4_words[:, :, cols].rearrange("a p c -> p a c").bitcast(I32))
+        def load_before(c):
+            befores[c] = sb("before%d" % c, [P, T2], F32, tag="tab_w%d" % (c % PASSES))
+            nc.sync.dma_start(befores[c][:], rows_of(page0, c))
+
+        def load_wgs(t):
+            for quad in range(4):
+                nc.sync.dma_start(wgs_sb[t][32 * quad : 32 * (quad + 1), :], wgs.rearrange("(q t) j -> t q j", t=PACK)[t])
 
         def load_table(a):
             nc.sync.dma_start(tab_w[a][:].bitcast(I32), tab_words[a].rearrange("p t i -> p (t i)").bitcast(I32))
@@ -98,44 +115,43 @@ def tile_list_facade_leakage_rounds_kernel(
                     scales[:, 4 * quad : 4 * quad + 4, :].rearrange("a q t -> q a t").bitcast(I32),
                 )
 
-        nc.gpsimd.memset(vec_rows[:], 0.0)
         nc.vector.memset(tab_s[:].rearrange("p a t -> p (a t)").bitcast(I32), 0)
-        nc.vector.memset(w4_s[:].rearrange("p a t -> p (a t)").bitcast(I32), 0)
-        nc.gpsimd.dma_start(vec_rows[0:TILES, :], gain.rearrange("(c p) -> c p", p=P))
+        nc.gpsimd.memset(w4_raw_s[:].rearrange("p a t -> p (a t)").bitcast(I32), 0)
         make_identity(nc, ident[:])
-        load_scales(nc.gpsimd, w4_s, w4_scales)
+        load_scales(nc.gpsimd, w4_raw_s, w4_scales)
         load_scales(nc.scalar, tab_s, tab_scales)
-        for tile, source in ((pick, offs), (put, offs2), (new_cols, offs3), (old_cols, offs4)):
-            nc.sync.dma_start(tile[:], source)
-        load_w4(slice(0, 2 * P))
+        nc.sync.dma_start(pick[:], offs)
+        load_wgs(0)
+        nc.sync.dma_start(w4_raw[:].bitcast(I32), w4_words.rearrange("a p c -> p a c").bitcast(I32))
         load_table(0)
-        nc.sync.dma_start(wgs_sb[:], wgs)
-        load_table(1)
+        nc.sync.dma_start(gain_cols[:], gain.rearrange("(a p t) -> p a t", a=PASSES, t=PACK))
         load_base(0)
+        load_table(1)
         load_page(0)
-        load_w4(slice(2 * P, 2 * H))
+        for tile, source in ((old_cols, offs4), (put, offs2), (new_cols, offs3)):
+            nc.sync.dma_start(tile[:], source)
         load_base(1)
+        load_wgs(1)
         load_page(1)
-        for c in range(2, BASE_BUFS):
-            load_page(c)
-            load_base(c)
+        load_base(2)
 
-        nc.tensor.transpose(xsum[0][:, 0:P], vec_rows[:], ident[:])
-        nc.scalar.copy(gain_cols[:], xsum[0][:, 0:TILES])
-        for c in range(TILES):
-            nc.scalar.activation(factors[c][:], wgs_sb[:], ACT.Copy, scale=gain_cols[:, c : c + 1])
-
+        nc.vector.tensor_copy(w4_w[:], w4_raw[:].rearrange("p a (b q t) -> p a b t q", b=PASSES, t=PACK))
         v_w = [sb("v_w0", [P, S], U32)]
         nc.vector.tensor_copy(v_w[0][:], tab_w[0][:].indirect(pick[:]))
         for a in range(PASSES):
             nc.vector.tensor_copy(v_s[:, a, :], tab_s[:, a, :].indirect(pick[:]))
+        dealt_s = w4_raw_s[:].rearrange("p a (b q t) -> p a b t q", b=PASSES, t=PACK)
+        nc.vector.tensor_copy(w4_s[:, :, 0, 0, :], dealt_s[:, :, 0, 0, :])
         v_w.append(sb("v_w1", [P, S], U32, tag="tab_s"))
         for h in range(2):
             nc.vector.tensor_copy(
                 v_w[1][:, h * BANK : (h + 1) * BANK], tab_w[1][:].indirect(pick[:, h * BANK // 16 : (h + 1) * BANK // 16])
             )
+        nc.vector.tensor_copy(w4_s[:, :, 0, 1:PACK, :], dealt_s[:, :, 0, 1:PACK, :])
+        nc.vector.tensor_copy(w4_s[:, :, 1, :, :], dealt_s[:, :, 1, :, :])
 
-        def add_transposed(bank, first, second, blocks):
+        def add_transposed(bank, first, second):
+            blocks = BANK // P
             for i, src in enumerate((first, second)):
                 for b in range(blocks):
                     cols = slice(b * P, (b + 1) * P)
@@ -147,146 +163,160 @@ def tile_list_facade_leakage_rounds_kernel(
         def half_cols(u):
             return slice((u % 2) * BANK, (u % 2 + 1) * BANK)
 
+        def entries(offsets, cols):
+            return offsets[:, cols.start // 16 : cols.stop // 16]
+
         def multiply(u):
             c, h = divmod(u, 2)
+            b, t = place(c)
             for a in range(PASSES):
                 nc.tensor.matmul_mx(
                     acc[h][:],
-                    lhsT=w4_w[:, a, 2 * c * P : 2 * (c + 1) * P].bitcast(FP4X4),
-                    lhsT_scale=w4_s[:, a, c * P : (c + 1) * P],
+                    lhsT=w4_w[:, a, b, t, :].bitcast(FP4X4),
+                    lhsT_scale=w4_s[:, a, b, t, :],
                     rhs=v_w[a][:, half_cols(u)].bitcast(FP8X4),
                     rhs_scale=v_s[:, a, half_cols(u)],
                     start=(a == 0), stop=(a == PASSES - 1),
                 )
             nc.scalar.copy(prod[h][:], acc[h][:])
-            add_transposed(summed[h], bases[c % BASE_BUFS][:, half_cols(u)], prod[h], 4)
+            add_transposed(summed[h], bases[c][:, half_cols(u)], prod[h])
 
         def reduce_range(u):
             h = u % 2
+            turns, minus_whole = terms[h][:, 0:BANK], terms[h][:, BANK : 2 * BANK]
             nc.scalar.activation(whole[h][:], summed[h][:], ACT.Copy, bias=ROUNDER, scale=0.5 / math.pi)
-            nc.scalar.activation(turns[h][:], summed[h][:], ACT.Copy, scale=0.5 / math.pi)
-            nc.scalar.activation(addend[h][:], whole[h][:], ACT.Copy, bias=ROUNDER, scale=-1.0)
-            add_transposed(reduced[h], turns[h], addend[h], 4)
+            nc.scalar.activation(turns, summed[h][:], ACT.Copy, scale=0.5 / math.pi)
+            nc.scalar.activation(minus_whole, whole[h][:], ACT.Copy, bias=ROUNDER, scale=-1.0)
+            add_transposed(reduced[h], turns, minus_whole)
 
         def take_sine(u):
             c, h = divmod(u, 2)
             nc.scalar.activation(sines[c % SINE_BUFS][:, half_cols(u)], reduced[h][:], ACT.Sin, scale=2.0 * math.pi)
 
-        def fetch_old(c):
-            nc.vector.tensor_copy(olds[:, c % OLD_BUFS, :], pages[c][:].indirect(old_cols[:]))
+        def make_factor(c):
+            a, t = place(c)
+            nc.scalar.activation(factors[c][:], wgs_sb[t][:], ACT.Copy, scale=gain_cols[:, a, t : t + 1])
 
         def put_new(c, cols):
             nc.vector.tensor_tensor(
-                pages[c][:].indirect(put[:, cols.start // 16 : cols.stop // 16]),
-                sines[c % SINE_BUFS][:, cols], factors[c][:, cols], MULT,
+                pages[c][:].indirect(entries(put, cols)), sines[c % SINE_BUFS][:, cols], factors[c][:, cols], MULT
             )
 
         def fetch_new(c, cols):
-            nc.vector.tensor_copy(factors[c][:, cols], pages[c][:].indirect(new_cols[:, cols.start // 16 : cols.stop // 16]))
+            nc.vector.tensor_copy(factors[c][:, cols], pages[c][:].indirect(entries(new_cols, cols)))
 
-        def round_x(c, q, sums):
-            rows = slice(32 * (c % TILES_A_PASS), 32 * (c % TILES_A_PASS) + 32)
-            nc.scalar.copy(x_t[q][:, :, :, rows, :], sums.rearrange("p (b i u e) -> p b u i e", b=2, u=2, e=2))
+        def x_rows(c, cols):
+            a, t = place(c)
+            return x_f[:, SPARE_X * a + t, cols]
 
-        def sum_x(u):
-            c, h = divmod(u, 2)
-            nc.scalar.activation(addend[h][:], factors[c][:, half_cols(u)], ACT.Abs)
-            add_transposed(xsum[h], addend[h], olds[:, c % OLD_BUFS, half_cols(u)], 4)
+        def add_old(c, cols, size):
+            nc.vector.tensor_tensor(x_rows(c, cols), befores[c][:].indirect(entries(old_cols, cols)), size, ADD)
 
-        def round_half(u):
-            c, h = divmod(u, 2)
-            for i in range(2):
-                round_x(c, 2 * h + i, xsum[h][:, i * CHUNK : (i + 1) * CHUNK])
+        def round_x(a, cols, copy):
+            copy(
+                x_g[:, cols, :].rearrange("p (c i) t -> p c t i", i=4),
+                x_f[:, SPARE_X * a : SPARE_X * a + PACK, cols].rearrange("p t (c i) -> p c t i", i=4),
+            )
 
-        def turn_x(q, bank, x_g, copy):
-            words = x_t[q][:].rearrange("p b u i e -> p (b u i e)").bitcast(F32)
-            for blk in range(4):
-                nc.tensor.transpose(bank[:, blk * P : (blk + 1) * P], words[:, blk * P : (blk + 1) * P], ident[:])
-            dst = x_g[:, q * CHUNK : (q + 1) * CHUNK, :].rearrange("p m t -> p (m t)").bitcast(F32)
-            copy(dst.rearrange("p (b m u) -> p b m u", b=2, u=2), bank[:].rearrange("p (b u m) -> p b m u", b=2, u=2))
-
-        def quantise_x(a, cols, x_g, x_w):
+        def quantise_x(a, cols):
             nc.vector.quantize_mx(
                 out=x_w[:, a, cols].bitcast(FP8X4), scales=x_s[:, a, cols], in_=x_g[:, cols, :].rearrange("p m t -> p (m t)")
             )
 
-        def quantise_w2():
-            raw = sb("w2_raw", [P, PASSES, 4, N], F32, tag="tab_w0")
-            for a in range(PASSES):
-                nc.sync.dma_start(raw[:, a, :, :], w2[a * BANK : (a + 1) * BANK, :].rearrange("(p t) n -> p t n", t=4))
-            for a in range(PASSES):
-                nc.scalar.copy(
-                    w2_g[a][:].rearrange("p (c i) t -> p c t i", i=4), raw[:, a, :, :].rearrange("p t (c i) -> p c t i", i=4)
-                )
-                nc.vector.quantize_mx(
-                    out=w2_w[:, a, :].bitcast(FP8X4), scales=w2_s[:, a, :], in_=w2_g[a][:].rearrange("p n t -> p (n t)")
-                )
+        def quantise_w2(a):
+            nc.scalar.copy(
+                w2_g[a][:].rearrange("p (c i) t -> p c t i", i=4), w2_raw[:, a, :, :].rearrange("p t (c i) -> p c t i", i=4)
+            )
+            nc.vector.quantize_mx(out=w2_w[:, a, :].bitcast(FP8X4), scales=w2_s[:, a, :], in_=w2_g[a][:].rearrange("p n t -> p (n t)"))
 
-        olds = sb("olds", [P, OLD_BUFS, M], F32, tag="tab_w1")
-        for c in range(OLD_BUFS):
-            fetch_old(c)
-        halves = 2 * TILES
+        every = slice(0, M)
+        chunks = [slice(q * CHUNK, (q + 1) * CHUNK) for q in range(CHUNKS)]
+        nc.vector.tensor_copy(x_rows(0, every), pages[0][:].indirect(old_cols[:]))
         for u in range(2):
             multiply(u)
             reduce_range(u)
+            if u == 0:
+                make_factor(0)
             take_sine(u)
             put_new(0, half_cols(u))
-        fetch_new(0, slice(0, M))
-        load_base(BASE_BUFS)
-        load_page(BASE_BUFS)
-        for u in range(halves + 2 * LAG - 1):
-            if u + 2 < halves:
+        fetch_new(0, every)
+        load_wgs(2)
+        load_page(2)
+        load_before(1)
+        load_base(3)
+        load_wgs(3)
+        load_page(3)
+        load_before(2)
+        for c in range(PACK, TILES):
+            load_base(c)
+        for a in range(PASSES):
+            nc.sync.dma_start(w2_raw[:, a, :, :], w2[a * BANK : (a + 1) * BANK, :].rearrange("(p t) n -> p t n", t=PACK))
+        with nc.allow_non_contiguous_dma(reason="one factor a partition"):
+            nc.sync.dma_start(sens_cols[:], sens.rearrange("(t p) -> p t", p=P))
+        load_page(PAGE_BUFS)
+
+        held = TILES - 3
+        for u in range(HALVES):
+            c = u // 2
+            behind = c - 2
+            if u % 2 == 1 and behind >= 0:
+                nc.scalar.activation(terms[1][:], factors[behind][:], ACT.Abs)
+                if behind == 0:
+                    nc.vector.tensor_tensor(x_rows(0, every), x_rows(0, every), terms[1][:], ADD)
+                elif behind < held:
+                    add_old(behind, every, terms[1][:])
+                    if behind + 2 < TILES - 1:
+                        load_before(behind + 2)
+            if u + 2 < HALVES:
                 multiply(u + 2)
-                if u % 2 == 1 and (u + 2) // 2 + BASE_BUFS < TILES:
-                    load_base((u + 2) // 2 + BASE_BUFS)
-                    load_page((u + 2) // 2 + BASE_BUFS)
-            if 2 <= u + 1 < halves:
+            if 2 <= u + 1 < HALVES:
                 reduce_range(u + 1)
-            if 2 <= u < halves:
+            if u >= 2:
                 take_sine(u)
-                if u % 2 == 1:
-                    put_new(u // 2, slice(0, S))
-                    if u // 2 < TILES - 1:
-                        fetch_new(u // 2, slice(0, M))
-            behind = u - 2 * LAG
-            if 0 <= behind - 1 < halves - 2:
-                round_half(behind - 1)
-                if (behind - 1) // 2 == TILES_A_PASS - 1:
-                    h = (behind - 1) % 2
-                    for i in range(2):
-                        turn_x(2 * h + i, xsum[h], x_g, nc.scalar.copy)
-                    if h == 1:
-                        quantise_x(0, slice(0, M), x_g, x_w)
-            if 0 <= behind < halves - 2:
-                sum_x(behind)
-                if behind % 2 == 1 and behind // 2 + OLD_BUFS < TILES:
-                    fetch_old(behind // 2 + OLD_BUFS)
-            if u == 2 * TILES_A_PASS - 1:
-                quantise_w2()
-                with nc.allow_non_contiguous_dma(reason="one factor a partition"):
-                    nc.sync.dma_start(sens_cols[:], sens.rearrange("(t p) -> p t", p=P))
+            if u % 2 == 0:
+                if c >= 1:
+                    make_factor(c)
+                if c == PACK - 1 or c == PACK:
+                    quantise_w2(c - PACK + 1)
+                if c == PACK + 2:
+                    for cols in chunks[0:2]:
+                        round_x(0, cols, nc.scalar.copy)
+                if c == PACK + 3:
+                    for cols in chunks[2:4]:
+                        round_x(0, cols, nc.scalar.copy)
+                    quantise_x(0, every)
+                continue
+            if c >= 1:
+                put_new(c, every)
+                if c < TILES - 1:
+                    fetch_new(c, every)
+                if c + PAGE_BUFS < TILES:
+                    load_page(c + PAGE_BUFS)
 
         last = TILES - 1
-        for q in range(CHUNKS):
-            fetch_new(last, slice(q * CHUNK, (q + 1) * CHUNK))
-        for q in range(CHUNKS):
-            cols = slice(q * CHUNK, (q + 1) * CHUNK)
-            size = addend[q // 2][:, (q % 2) * CHUNK : (q % 2 + 1) * CHUNK]
-            nc.scalar.activation(size, factors[last][:, cols], ACT.Abs)
-            add_transposed(xsum[q % 2], olds[:, last % OLD_BUFS, cols], size, 2)
-            round_x(last, q, xsum[q % 2][:, 0:CHUNK])
-            turn_x(q, reduced[q % 2], x_g, nc.vector.tensor_copy)
-            quantise_x(1, cols, x_g, x_w)
-        for q in range(CHUNKS):
-            cols = slice(q * CHUNK, (q + 1) * CHUNK)
-            staged = sines[q % 2]
+        befores[last] = sb("before%d" % last, [P, T2], F32, tag="page0")
+        nc.sync.dma_start(befores[last][:], rows_of(page0, last))
+        nc.scalar.activation(terms[0][:], factors[last - 1][:], ACT.Abs)
+        pieces = chunks[:-1] + [slice(M - CHUNK, M - P), slice(M - P, M)]
+        for q, cols in enumerate(pieces):
+            if q < CHUNKS:
+                fetch_new(last, chunks[q])
+                nc.scalar.activation(factors[last - 1][:, chunks[q]], factors[last][:, chunks[q]], ACT.Abs)
+            add_old(last - 2, cols, terms[1][:, cols])
+            add_old(last - 1, cols, terms[0][:, cols])
+            add_old(last, cols, factors[last - 1][:, cols])
+            round_x(1, cols, nc.scalar.copy if q < 2 else nc.vector.tensor_copy)
+            quantise_x(1, cols)
+        for q, cols in enumerate(pieces):
+            width = cols.stop - cols.start
+            staged = sines[q % SINE_BUFS]
             for pair in range(2):
-                bank = banks[2 * (q % 2) + pair]
+                bank = banks[2 * (q % 4) + pair]
                 for a in range(PASSES):
                     for i in range(2):
                         n_cols = slice((2 * pair + i) * P, (2 * pair + i + 1) * P)
                         nc.tensor.matmul_mx(
-                            bank[:, i * CHUNK : (i + 1) * CHUNK],
+                            bank[:, i * width : (i + 1) * width],
                             lhsT=w2_w[:, a, n_cols].bitcast(FP8X4),
                             lhsT_scale=w2_s[:, a, n_cols],
                             rhs=x_w[:, a, cols].bitcast(FP8X4),
@@ -296,10 +326,10 @@ def tile_list_facade_leakage_rounds_kernel(
                 for i in range(2):
                     nt = 2 * pair + i
                     nc.scalar.activation(
-                        staged[:, nt * CHUNK : (nt + 1) * CHUNK], bank[:, i * CHUNK : (i + 1) * CHUNK], ACT.Tanh,
+                        staged[:, nt * width : (nt + 1) * width], bank[:, i * width : (i + 1) * width], ACT.Tanh,
                         scale=sens_cols[:, nt : nt + 1],
                     )
                 nc.sync.dma_start(
                     out[2 * pair * P : 2 * (pair + 1) * P, cols].rearrange("(i p) m -> p i m", p=P),
-                    staged[:, 2 * pair * CHUNK : 2 * (pair + 1) * CHUNK].rearrange("p (i m) -> p i m", i=2),
+                    staged[:, 2 * pair * width : 2 * (pair + 1) * width].rearrange("p (i m) -> p i m", i=2),
                 )

@@ -115,11 +115,14 @@ def tile_list_facade_leakage_rounds_kernel(
                     scales[:, 4 * quad : 4 * quad + 4, :].rearrange("a q t -> q a t").bitcast(I32),
                 )
 
+        warm = sb("warm", [P, 8], F32)
+        nc.gpsimd.memset(warm[:, 0:1], 0.0)
         nc.vector.memset(tab_s[:].rearrange("p a t -> p (a t)").bitcast(I32), 0)
         nc.gpsimd.memset(w4_raw_s[:].rearrange("p a t -> p (a t)").bitcast(I32), 0)
         make_identity(nc, ident[:])
         load_scales(nc.gpsimd, w4_raw_s, w4_scales)
         load_scales(nc.scalar, tab_s, tab_scales)
+        nc.scalar.activation(warm[:, 1:2], warm[:, 0:1], ACT.Silu)
         nc.sync.dma_start(pick[:], offs)
         load_wgs(0)
         nc.sync.dma_start(w4_raw[:].bitcast(I32), w4_words.rearrange("a p c -> p a c").bitcast(I32))
@@ -223,11 +226,16 @@ def tile_list_facade_leakage_rounds_kernel(
                 out=x_w[:, a, cols].bitcast(FP8X4), scales=x_s[:, a, cols], in_=x_g[:, cols, :].rearrange("p m t -> p (m t)")
             )
 
-        def quantise_w2(a):
+        def quantise_w2(piece):
+            a, cols = piece // 2, slice((piece % 2) * N // 2, (piece % 2 + 1) * N // 2)
             nc.scalar.copy(
-                w2_g[a][:].rearrange("p (c i) t -> p c t i", i=4), w2_raw[:, a, :, :].rearrange("p t (c i) -> p c t i", i=4)
+                w2_g[a][:, cols, :].rearrange("p (c i) t -> p c t i", i=4),
+                w2_raw[:, a, :, cols].rearrange("p t (c i) -> p c t i", i=4),
             )
-            nc.vector.quantize_mx(out=w2_w[:, a, :].bitcast(FP8X4), scales=w2_s[:, a, :], in_=w2_g[a][:].rearrange("p n t -> p (n t)"))
+            if piece % 2 == 1:
+                nc.vector.quantize_mx(
+                    out=w2_w[:, a, :].bitcast(FP8X4), scales=w2_s[:, a, :], in_=w2_g[a][:].rearrange("p n t -> p (n t)")
+                )
 
         every = slice(0, M)
         chunks = [slice(q * CHUNK, (q + 1) * CHUNK) for q in range(CHUNKS)]
@@ -247,10 +255,10 @@ def tile_list_facade_leakage_rounds_kernel(
         load_wgs(3)
         load_page(3)
         load_before(2)
-        for c in range(PACK, TILES):
-            load_base(c)
         for a in range(PASSES):
             nc.sync.dma_start(w2_raw[:, a, :, :], w2[a * BANK : (a + 1) * BANK, :].rearrange("(p t) n -> p t n", t=PACK))
+        for c in range(PACK, TILES):
+            load_base(c)
         with nc.allow_non_contiguous_dma(reason="one factor a partition"):
             nc.sync.dma_start(sens_cols[:], sens.rearrange("(t p) -> p t", p=P))
         load_page(PAGE_BUFS)
@@ -273,25 +281,19 @@ def tile_list_facade_leakage_rounds_kernel(
                 reduce_range(u + 1)
             if u >= 2:
                 take_sine(u)
-            if u % 2 == 0:
-                if c >= 1:
-                    make_factor(c)
-                if c == PACK - 1 or c == PACK:
-                    quantise_w2(c - PACK + 1)
-                if c == PACK + 2:
-                    for cols in chunks[0:2]:
-                        round_x(0, cols, nc.scalar.copy)
-                if c == PACK + 3:
-                    for cols in chunks[2:4]:
-                        round_x(0, cols, nc.scalar.copy)
-                    quantise_x(0, every)
-                continue
-            if c >= 1:
+            if u % 2 == 0 and c >= 1:
+                make_factor(c)
+            if u % 2 == 1 and c >= 1:
                 put_new(c, every)
                 if c < TILES - 1:
                     fetch_new(c, every)
                 if c + PAGE_BUFS < TILES:
                     load_page(c + PAGE_BUFS)
+            if HALVES - 2 * CHUNKS - 1 <= u < HALVES - CHUNKS - 1:
+                quantise_w2(u - (HALVES - 2 * CHUNKS - 1))
+            if u >= HALVES - CHUNKS:
+                round_x(0, chunks[u - (HALVES - CHUNKS)], nc.scalar.copy)
+        quantise_x(0, every)
 
         last = TILES - 1
         befores[last] = sb("before%d" % last, [P, T2], F32, tag="page0")

import math
from contextlib import ExitStack

import concourse.mybir as mybir
from concourse.masks import make_identity

K, T, H, S, T2, M, N = 1024, 4096, 1024, 1024, 2048, 1024, 512
FLOPS = 2 * K * H * S + 2 * H * N * M

F32 = mybir.dt.float32
BF16 = mybir.dt.bfloat16
I32 = mybir.dt.int32
U32 = mybir.dt.uint32
U16 = mybir.dt.uint16
U8 = mybir.dt.uint8
FP8X4 = mybir.dt.float8_e4m3fn_x4
FP4X4 = mybir.dt.float4_e2m1fn_x4
ACT = mybir.ActivationFunctionType
MULT = mybir.AluOpType.mult
ADD = mybir.AluOpType.add

P = 128
BANK = 512
PASSES = 2
PACK = 4
TILES = PASSES * PACK
HALVES = 2 * TILES
N_TILES = N // P
CHUNK = 256
CHUNKS = M // CHUNK
ROUNDER = 12582912.0
PAGE_BUFS = 4
SINE_BUFS = 3
SPARE_X = 2


def place(c):
    a = c // PACK
    return a, (c + SPARE_X * a) % PACK


def tile_list_facade_leakage_rounds_kernel(
    tc, tab_words, tab_scales, offs, w4_words, w4_scales, base, gain, wgs, page0, offs2, offs3, offs4, w2, sens, out
):
    nc = tc.nc
    with ExitStack() as ctx:
        lists = ctx.enter_context(tc.tile_pool(name="lists", bufs=1))
        keep = ctx.enter_context(tc.tile_pool(name="keep", bufs=1))
        psum = ctx.enter_context(tc.psum_pool(name="psum", bufs=1))

        def sb(name, shape, dtype, tag=""):
            return keep.tile(shape, dtype, name=name, tag=tag or name, align_bytes=64)

        pick = lists.tile([P, S // 16], U16, name="pick")
        put = lists.tile([P, S // 16], U16, name="put")
        new_cols = lists.tile([P, M // 16], U16, name="new_cols")
        old_cols = lists.tile([P, M // 16], U16, name="old_cols")

        banks = [psum.tile([P, BANK], F32, name="bank%d" % b, tag="bank%d" % b) for b in range(8)]
        acc, summed, reduced = banks[0:2], banks[2:4], banks[4:6]

        tab_w = [sb("tab_w%d" % a, [P, T], U32) for a in range(PASSES)]
        tab_s = sb("tab_s", [P, PASSES, T], U8)
        v_s = sb("v_s", [P, PASSES, S], U8)
        w4_raw = sb("w4_raw", [P, PASSES, H], U16)
        w4_raw_s = sb("w4_raw_s", [P, PASSES, H], U8)
        w4_w = sb("w4_w", [P, PASSES, PASSES, PACK, P], U16)
        w4_s = sb("w4_s", [P, PASSES, PASSES, PACK, P], U8)
        ident = sb("ident", [P, P], F32)
        gain_cols = sb("gain_cols", [P, PASSES, PACK], F32)
        sens_cols = sb("sens_cols", [P, N_TILES], F32)
        wgs_sb = [sb("wgs%d" % t, [P, S], F32) for t in range(PACK)]
        factors = [sb("factor%d" % c, [P, S], F32) for c in range(TILES)]
        sines = [sb("sine%d" % b, [P, S], F32) for b in range(SINE_BUFS)]
        bases = [sines[SINE_BUFS - 1]] + factors[1:]
        prod = [sb("prod%d" % h, [P, BANK], F32) for h in range(2)]
        whole = [sb("whole%d" % h, [P, BANK], U32) for h in range(2)]
        terms = [sb("terms%d" % h, [P, 2 * BANK], F32) for h in range(2)]
        x_f = sb("x_f", [P, PACK + SPARE_X, M], F32)
        x_g = sb("x_g", [P, M, PACK], BF16)
        x_w = sb("x_w", [P, PASSES, M], U32)
        x_s = sb("x_s", [P, PASSES, M], U8)
        w2_raw = sb("w2_raw", [P, PASSES, PACK, N], F32)
        w2_g = [sb("w2_g%d" % a, [P, N, PACK], BF16) for a in range(PASSES)]
        w2_w = sb("w2_w", [P, PASSES, N], U32)
        w2_s = sb("w2_s", [P, PASSES, N], U8)
        pages, befores = {}, {}

        def rows_of(matrix, c):
            a, t = place(c)
            return matrix.rearrange("(a p t) j -> a t p j", a=PASSES, t=PACK)[a, t]

        def load_base(c):
            nc.sync.dma_start(bases[c][:], rows_of(base, c))

        def load_page(c):
            pages[c] = sb("page%d" % c, [P, T2], F32, tag="page%d" % (c % PAGE_BUFS))
            nc.sync.dma_start(pages[c][:], rows_of(page0, c))

        def load_before(c):
            befores[c] = sb("before%d" % c, [P, T2], F32, tag="tab_w%d" % (c % PASSES))
            nc.sync.dma_start(befores[c][:], rows_of(page0, c))

        def load_wgs(t):
            for quad in range(4):
                nc.sync.dma_start(wgs_sb[t][32 * quad : 32 * (quad + 1), :], wgs.rearrange("(q t) j -> t q j", t=PACK)[t])

        def load_table(a):
            nc.sync.dma_start(tab_w[a][:].bitcast(I32), tab_words[a].rearrange("p t i -> p (t i)").bitcast(I32))

        def load_scales(queue, scales_sb, scales):
            for quad in range(4):
                queue.dma_start(
                    scales_sb[32 * quad : 32 * quad + 4, :, :].bitcast(I32),
                    scales[:, 4 * quad : 4 * quad + 4, :].rearrange("a q t -> q a t").bitcast(I32),
                )

        warm = sb("warm", [P, 8], F32)
        nc.gpsimd.memset(warm[:, 0:1], 0.0)
        nc.vector.memset(tab_s[:].rearrange("p a t -> p (a t)").bitcast(I32), 0)
        nc.gpsimd.memset(w4_raw_s[:].rearrange("p a t -> p (a t)").bitcast(I32), 0)
        make_identity(nc, ident[:])
        load_scales(nc.gpsimd, w4_raw_s, w4_scales)
        load_scales(nc.scalar, tab_s, tab_scales)
        nc.scalar.activation(warm[:, 1:2], warm[:, 0:1], ACT.Silu)
        nc.sync.dma_start(pick[:], offs)
        load_wgs(0)
        nc.sync.dma_start(w4_raw[:].bitcast(I32), w4_words.rearrange("a p c -> p a c").bitcast(I32))
        load_table(0)
        nc.sync.dma_start(gain_cols[:], gain.rearrange("(a p t) -> p a t", a=PASSES, t=PACK))
        load_base(0)
        load_table(1)
        load_page(0)
        for tile, source in ((old_cols, offs4), (put, offs2), (new_cols, offs3)):
            nc.sync.dma_start(tile[:], source)
        load_base(1)
        load_wgs(1)
        load_page(1)
        load_base(2)

        nc.vector.tensor_copy(w4_w[:], w4_raw[:].rearrange("p a (b q t) -> p a b t q", b=PASSES, t=PACK))
        v_w = [sb("v_w0", [P, S], U32)]
        nc.vector.tensor_copy(v_w[0][:], tab_w[0][:].indirect(pick[:]))
        for a in range(PASSES):
            nc.vector.tensor_copy(v_s[:, a, :], tab_s[:, a, :].indirect(pick[:]))
        dealt_s = w4_raw_s[:].rearrange("p a (b q t) -> p a b t q", b=PASSES, t=PACK)
        nc.vector.tensor_copy(w4_s[:, :, 0, 0, :], dealt_s[:, :, 0, 0, :])
        v_w.append(sb("v_w1", [P, S], U32, tag="tab_s"))
        for h in range(2):
            nc.vector.tensor_copy(
                v_w[1][:, h * BANK : (h + 1) * BANK], tab_w[1][:].indirect(pick[:, h * BANK // 16 : (h + 1) * BANK // 16])
            )
        nc.vector.tensor_copy(w4_s[:, :, 0, 1:PACK, :], dealt_s[:, :, 0, 1:PACK, :])
        nc.vector.tensor_copy(w4_s[:, :, 1, :, :], dealt_s[:, :, 1, :, :])

        def add_transposed(bank, first, second):
            blocks = BANK // P
            for i, src in enumerate((first, second)):
                for b in range(blocks):
                    cols = slice(b * P, (b + 1) * P)
                    nc.tensor.matmul(
                        bank[:, cols], src[:, cols], ident[:], is_transpose=True,
                        start=(i == 0 and b == 0), stop=(i == 1 and b == blocks - 1),
                    )

        def half_cols(u):
            return slice((u % 2) * BANK, (u % 2 + 1) * BANK)

        def entries(offsets, cols):
            return offsets[:, cols.start // 16 : cols.stop // 16]

        def multiply(u):
            c, h = divmod(u, 2)
            b, t = place(c)
            for a in range(PASSES):
                nc.tensor.matmul_mx(
                    acc[h][:],
                    lhsT=w4_w[:, a, b, t, :].bitcast(FP4X4),
                    lhsT_scale=w4_s[:, a, b, t, :],
                    rhs=v_w[a][:, half_cols(u)].bitcast(FP8X4),
                    rhs_scale=v_s[:, a, half_cols(u)],
                    start=(a == 0), stop=(a == PASSES - 1),
                )
            nc.scalar.copy(prod[h][:], acc[h][:])
            add_transposed(summed[h], bases[c][:, half_cols(u)], prod[h])

        def reduce_range(u):
            h = u % 2
            turns, minus_whole = terms[h][:, 0:BANK], terms[h][:, BANK : 2 * BANK]
            nc.scalar.activation(whole[h][:], summed[h][:], ACT.Copy, bias=ROUNDER, scale=0.5 / math.pi)
            nc.scalar.activation(turns, summed[h][:], ACT.Copy, scale=0.5 / math.pi)
            nc.scalar.activation(minus_whole, whole[h][:], ACT.Copy, bias=ROUNDER, scale=-1.0)
            add_transposed(reduced[h], turns, minus_whole)

        def take_sine(u):
            c, h = divmod(u, 2)
            nc.scalar.activation(sines[c % SINE_BUFS][:, half_cols(u)], reduced[h][:], ACT.Sin, scale=2.0 * math.pi)

        def make_factor(c):
            a, t = place(c)
            nc.scalar.activation(factors[c][:], wgs_sb[t][:], ACT.Copy, scale=gain_cols[:, a, t : t + 1])

        def put_new(c, cols):
            nc.vector.tensor_tensor(
                pages[c][:].indirect(entries(put, cols)), sines[c % SINE_BUFS][:, cols], factors[c][:, cols], MULT
            )

        def fetch_new(c, cols):
            nc.vector.tensor_copy(factors[c][:, cols], pages[c][:].indirect(entries(new_cols, cols)))

        def x_rows(c, cols):
            a, t = place(c)
            return x_f[:, SPARE_X * a + t, cols]

        def add_old(c, cols, size):
            nc.vector.tensor_tensor(x_rows(c, cols), befores[c][:].indirect(entries(old_cols, cols)), size, ADD)

        def round_x(a, cols, copy):
            copy(
                x_g[:, cols, :].rearrange("p (c i) t -> p c t i", i=4),
                x_f[:, SPARE_X * a : SPARE_X * a + PACK, cols].rearrange("p t (c i) -> p c t i", i=4),
            )

        def quantise_x(a, cols):
            nc.vector.quantize_mx(
                out=x_w[:, a, cols].bitcast(FP8X4), scales=x_s[:, a, cols], in_=x_g[:, cols, :].rearrange("p m t -> p (m t)")
            )

        def quantise_w2(piece):
            a, cols = piece // 2, slice((piece % 2) * N // 2, (piece % 2 + 1) * N // 2)
            nc.scalar.copy(
                w2_g[a][:, cols, :].rearrange("p (c i) t -> p c t i", i=4),
                w2_raw[:, a, :, cols].rearrange("p t (c i) -> p c t i", i=4),
            )
            if piece % 2 == 1:
                nc.vector.quantize_mx(
                    out=w2_w[:, a, :].bitcast(FP8X4), scales=w2_s[:, a, :], in_=w2_g[a][:].rearrange("p n t -> p (n t)")
                )

        every = slice(0, M)
        chunks = [slice(q * CHUNK, (q + 1) * CHUNK) for q in range(CHUNKS)]
        nc.vector.tensor_copy(x_rows(0, every), pages[0][:].indirect(old_cols[:]))
        for u in range(2):
            multiply(u)
            reduce_range(u)
            if u == 0:
                make_factor(0)
            take_sine(u)
            put_new(0, half_cols(u))
        fetch_new(0, every)
        load_wgs(2)
        load_page(2)
        load_before(1)
        load_base(3)
        load_wgs(3)
        load_page(3)
        load_before(2)
        for a in range(PASSES):
            nc.sync.dma_start(w2_raw[:, a, :, :], w2[a * BANK : (a + 1) * BANK, :].rearrange("(p t) n -> p t n", t=PACK))
        for c in range(PACK, TILES):
            load_base(c)
        with nc.allow_non_contiguous_dma(reason="one factor a partition"):
            nc.sync.dma_start(sens_cols[:], sens.rearrange("(t p) -> p t", p=P))
        load_page(PAGE_BUFS)

        held = TILES - 3
        for u in range(HALVES):
            c = u // 2
            behind = c - 2
            if u % 2 == 1 and behind >= 0:
                nc.scalar.activation(terms[1][:], factors[behind][:], ACT.Abs)
                if behind == 0:
                    nc.vector.tensor_tensor(x_rows(0, every), x_rows(0, every), terms[1][:], ADD)
                elif behind < held:
                    add_old(behind, every, terms[1][:])
                    if behind + 2 < TILES - 1:
                        load_before(behind + 2)
            if u + 2 < HALVES:
                multiply(u + 2)
            if 2 <= u + 1 < HALVES:
                reduce_range(u + 1)
            if u >= 2:
                take_sine(u)
            if u % 2 == 0 and c >= 1:
                make_factor(c)
            if u % 2 == 1 and c >= 1:
                put_new(c, every)
                if c < TILES - 1:
                    fetch_new(c, every)
                if c + PAGE_BUFS < TILES:
                    load_page(c + PAGE_BUFS)
            if HALVES - 2 * CHUNKS - 1 <= u < HALVES - CHUNKS - 1:
                quantise_w2(u - (HALVES - 2 * CHUNKS - 1))
            if u >= HALVES - CHUNKS:
                round_x(0, chunks[u - (HALVES - CHUNKS)], nc.scalar.copy)
        quantise_x(0, every)

        last = TILES - 1
        befores[last] = sb("before%d" % last, [P, T2], F32, tag="page0")
        nc.sync.dma_start(befores[last][:], rows_of(page0, last))
        nc.scalar.activation(terms[0][:], factors[last - 1][:], ACT.Abs)
        pieces = chunks[:-1] + [slice(M - CHUNK, M - P), slice(M - P, M)]
        for q, cols in enumerate(pieces):
            if q < CHUNKS:
                fetch_new(last, chunks[q])
                nc.scalar.activation(factors[last - 1][:, chunks[q]], factors[last][:, chunks[q]], ACT.Abs)
            add_old(last - 2, cols, terms[1][:, cols])
            add_old(last - 1, cols, terms[0][:, cols])
            add_old(last, cols, factors[last - 1][:, cols])
            round_x(1, cols, nc.scalar.copy if q < 2 else nc.vector.tensor_copy)
            quantise_x(1, cols)
        for q, cols in enumerate(pieces):
            width = cols.stop - cols.start
            staged = sines[q % SINE_BUFS]
            for pair in range(2):
                bank = banks[2 * (q % 4) + pair]
                for a in range(PASSES):
                    for i in range(2):
                        n_cols = slice((2 * pair + i) * P, (2 * pair + i + 1) * P)
                        nc.tensor.matmul_mx(
                            bank[:, i * width : (i + 1) * width],
                            lhsT=w2_w[:, a, n_cols].bitcast(FP8X4),
                            lhsT_scale=w2_s[:, a, n_cols],
                            rhs=x_w[:, a, cols].bitcast(FP8X4),
                            rhs_scale=x_s[:, a, cols],
                            start=(a == 0 and i == 0), stop=(a == PASSES - 1 and i == 1),
                        )
                for i in range(2):
                    nt = 2 * pair + i
                    nc.scalar.activation(
                        staged[:, nt * width : (nt + 1) * width], bank[:, i * width : (i + 1) * width], ACT.Tanh,
                        scale=sens_cols[:, nt : nt + 1],
                    )
                nc.sync.dma_start(
                    out[2 * pair * P : 2 * (pair + 1) * P, cols].rearrange("(i p) m -> p i m", p=P),
                    staged[:, 2 * pair * width : 2 * (pair + 1) * width].rearrange("p (i m) -> p i m", i=2),
                )
